import numpy as np
import ml_dtypes


def mxq(x, axis, fmt="e4m3"):
    dtype, down = {"e4m3": (ml_dtypes.float8_e4m3fn, 7), "e5m2": (ml_dtypes.float8_e5m2, 14)}[fmt]
    v = np.moveaxis(np.asarray(x, np.float32).astype(ml_dtypes.bfloat16).astype(np.float64), axis, -1)
    blocks = v.reshape(v.shape[:-1] + (-1, 32))
    amax = np.abs(blocks).max(-1, keepdims=True)
    byte = np.maximum(np.where(amax > 0, np.frexp(amax)[1] - 1 + 127, 0) - down, 1)
    scale = np.exp2(byte - 127.0)
    codes = (blocks / scale).astype(np.float32).astype(dtype).astype(np.float64)
    return np.moveaxis((codes * scale).reshape(v.shape), -1, axis)


WIDE = False


def mx_kscale(k):
    if not WIDE:
        return np.ones(k)
    levels = np.array([10, -10, 5, -5, 0])
    if k % 512:
        return np.exp2(np.random.permutation(np.resize(levels, k // 32))).repeat(32)
    a = np.empty((k // 512, 16))
    for p in range(k // 512):
        a[p, :8] = np.random.permutation(np.resize(levels, 8))
        for g in range(8):
            far = levels[np.abs(levels - a[p, g]) >= 10]
            a[p, g + 8] = far[np.random.randint(len(far))]
    return np.exp2(a.ravel()).repeat(32)


def f64(x):
    return np.asarray(x).astype(np.float64)


def striped8(idx):
    return np.concatenate([v.reshape(-1, 16).T for v in idx]).astype(np.uint16)


def unstriped8(offs):
    return np.stack([offs[16 * g:16 * g + 16].T.reshape(-1) for g in range(8)]).astype(np.int64)


E2M1 = np.array([0.0, 0.5, 1.0, 1.5, 2.0, 3.0, 4.0, 6.0, -0.0, -0.5, -1.0, -1.5, -2.0, -3.0, -4.0, -6.0])


def pack_weight(w, fmt):
    k, n = w.shape
    w = f64(np.asarray(w, np.float32).astype(ml_dtypes.bfloat16)).reshape(k // 32, 32, n)
    amax = np.abs(w).max(1)
    if fmt == "e4m3":
        byte = np.frexp(amax)[1] - 1 + 127 - 7
    else:
        mant, ex = np.frexp(amax / 6.0)
        byte = np.where(mant > 0.5, ex, ex - 1) + 127
    byte = np.clip(np.where(amax > 0, byte, 1), 1, 254)
    scaled = (w * np.exp2(127.0 - byte)[:, None, :]).reshape(k, n).astype(np.float32)
    by_word = np.ascontiguousarray(scaled.reshape(k // 512, 128, 4, n).transpose(0, 1, 3, 2))
    if fmt == "e4m3":
        words = by_word.astype(ml_dtypes.float8_e4m3fn).view(np.uint8)
    else:
        c = by_word.astype(ml_dtypes.float4_e2m1fn).view(np.uint8) & 0xF
        words = (c[..., 0::2] | (c[..., 1::2] << 4)).reshape(k // 512, 128, 2 * n)
    return np.ascontiguousarray(words), np.ascontiguousarray(byte.astype(np.uint8).reshape(k // 512, 16, n))


def unpack_weight(words, scales, fmt):
    g, _, n = scales.shape
    words = np.ascontiguousarray(words).reshape(g, 128, n, -1)
    if fmt == "e4m3":
        vals = words.view(ml_dtypes.float8_e4m3fn).astype(np.float64)
    else:
        nib = np.empty((g, 128, n, 4), np.uint8)
        nib[..., 0::2] = words & 0xF
        nib[..., 1::2] = words >> 4
        vals = E2M1[nib]
    vals = vals * np.repeat(np.exp2(scales.astype(np.float64) - 127.0), 8, axis=1)[..., None]
    return vals.transpose(0, 1, 3, 2).reshape(g * 512, n)


K, M, T, S = 512, 128, 4096, 2048


def setup_inputs():
    n = np.random.standard_normal
    s = mx_kscale(K)[:, None]
    p_w = pack_weight(n((K, M)) / np.sqrt(K) / s, "e2m1")
    return {
        "x": (n((K, S)) * s).astype(np.float32),
        "w_words": p_w[0],
        "w_scales": p_w[1],
        "b": (0.3 * n(128)).astype(np.float32),
        "wgo": np.repeat(np.random.uniform(0.5, 2.0, (8, S)), 16, axis=0).astype(np.float32),
        "offs": striped8(np.stack([np.random.permutation(T)[:S] for _ in range(8)])),
    }


def reference(x, w_words, w_scales, b, wgo, offs):
    x_ = mxq(f64(x), 0, "e4m3")
    w_ = unpack_weight(w_words, w_scales, "e2m1")
    y = w_.T @ x_
    place = unstriped8(offs)[np.arange(M) % 128 // 16]
    out = np.zeros((M, T))
    out[np.arange(M)[:, None], place] = f64(wgo)[np.arange(M) % 128] * (y + f64(b)[:, None])
    return out

@@ -1,0 +1,128 @@
+from contextlib import ExitStack
+
+import concourse.mybir as mybir
+
+FLOPS = 2 * 512 * 128 * 2048
+
+F32 = mybir.dt.float32
+BF16 = mybir.dt.bfloat16
+U32 = mybir.dt.uint32
+I32 = mybir.dt.int32
+U16 = mybir.dt.uint16
+U8 = mybir.dt.uint8
+FP8X4 = mybir.dt.float8_e4m3fn_x4
+FP4X4 = mybir.dt.float4_e2m1fn_x4
+MULT = mybir.AluOpType.mult
+IDENTITY = mybir.ActivationFunctionType.Identity
+
+P = 128
+PACK = 4
+S = 2048
+T = 4096
+HALF = S // 2
+
+LOADS = (((0, 512), (512, 256), (768, 256)), ((1024, 512), (1536, 256), (1792, 256)))
+PIECES = (
+    ((0, 256, "v"), (256, 256, "s"), (512, 128, "v"), (640, 128, "s"), (768, 128, "v"), (896, 128, "s")),
+    ((1024, 256, "s"), (1280, 256, "s"), (1536, 256, "s"), (1792, 256, "s")),
+)
+
+
+def tile_list_hscat_bias_kernel(tc, x, w_words, w_scales, b, wgo, offs, out):
+    nc = tc.nc
+    with ExitStack() as ctx:
+        held = ctx.enter_context(tc.tile_pool(name="held", bufs=1))
+        psum = ctx.enter_context(tc.psum_pool(name="psum", bufs=8))
+
+        offsets = held.tile([P, S // 16], U16, name="offsets")
+        window = held.tile([P, T], F32, name="window")
+        w_codes = held.tile([P, 2 * P], U8, name="w_codes", align_bytes=64)
+        w_plane = held.tile([P, P], U8, name="w_plane", align_bytes=64)
+        b_col = held.tile([P, 1], F32, name="b_col")
+        warm = held.tile([P, 1], F32, name="warm")
+
+        x_view = x.rearrange("(p j) s -> p j s", j=PACK)
+        raw = {}
+
+        def load_x(first, tokens):
+            chunk = held.tile([P, PACK, tokens], F32, name="raw_%d" % first)
+            nc.sync.dma_start(out=chunk[:], in_=x_view[:, :, first : first + tokens])
+            raw[first] = (chunk, tokens)
+
+        nc.gpsimd.memset(w_plane[:].bitcast(I32), 0)
+        nc.gpsimd.dma_start(out=b_col[:], in_=b.rearrange("(p o) -> p o", o=1))
+        nc.vector.memset(warm[:], 0.0)
+        nc.scalar.dma_start(out=w_codes[:].bitcast(I32), in_=w_words[0].bitcast(I32))
+        for q in range(4):
+            nc.scalar.dma_start(
+                out=w_plane[32 * q : 32 * q + 4, :].bitcast(I32), in_=w_scales[0, 4 * q : 4 * q + 4, :].bitcast(I32)
+            )
+        nc.scalar.activation(warm[:], warm[:], IDENTITY)
+        nc.vector.memset(window[:], 0.0)
+        for load in LOADS[0]:
+            load_x(*load)
+        nc.sync.dma_start(offsets[:], offs)
+        wgo_tiles = []
+        for h in range(2):
+            if h == 1:
+                for load in LOADS[1]:
+                    load_x(*load)
+            wgo_half = held.tile([P, HALF], F32, name="wgo_%d" % h)
+            nc.sync.dma_start(out=wgo_half[:], in_=wgo[:, h * HALF : (h + 1) * HALF])
+            wgo_tiles.append(wgo_half)
+
+        def interleave(first, tokens, engine):
+            base = max(c for c in raw if c <= first)
+            chunk = raw[base][0]
+            grouped = held.tile([P, tokens * PACK], BF16, name="grouped_%d" % first, align_bytes=64)
+            dst = grouped[:].rearrange("p (c i t) -> p c t i", i=4, t=PACK)
+            src = chunk[:, :, first - base : first - base + tokens].rearrange("p t (c i) -> p c t i", i=4)
+            if engine == "v":
+                nc.vector.tensor_copy(out=dst, in_=src)
+            else:
+                nc.scalar.copy(out=dst, in_=src)
+            return grouped
+
+        def multiply(first, tokens, grouped, y, column):
+            codes = held.tile([P, tokens], U32, name="codes_%d" % first, align_bytes=64)
+            plane = held.tile([P, tokens], U8, name="plane_%d" % first, align_bytes=64)
+            nc.vector.quantize_mx(out=codes[:].bitcast(FP8X4), scales=plane[:], in_=grouped[:])
+            acc = psum.tile([P, 512], F32, name="acc")
+            nc.tensor.matmul_mx(
+                out=acc[:, 0:tokens],
+                lhsT=w_codes[:].bitcast(FP4X4),
+                lhsT_scale=w_plane[:],
+                rhs=codes[:].bitcast(FP8X4),
+                rhs_scale=plane[:],
+                start=True,
+                stop=True,
+            )
+            nc.scalar.activation(y[:, column : column + tokens], acc[:, 0:tokens], IDENTITY, bias=b_col[:])
+
+        def interleave_all(pieces):
+            return [interleave(*piece) for piece in pieces]
+
+        def multiply_all(pieces, grouped, y, h):
+            for (first, tokens, engine), tile in zip(pieces, grouped):
+                multiply(first, tokens, tile, y, first - h * HALF)
+
+        def scatter(y, h):
+            nc.vector.tensor_tensor(
+                window[:].indirect(offsets[:, h * 64 : (h + 1) * 64]), y[:], wgo_tiles[h][:], MULT
+            )
+
+        y_0 = held.tile([P, HALF], F32, name="y_0")
+        y_1 = held.tile([P, HALF], F32, name="y_1")
+        early, late = PIECES[0][:4], PIECES[0][4:]
+        grouped_early = interleave_all(early)
+        multiply_all(early[:2], grouped_early[:2], y_0, 0)
+        grouped_late = interleave_all(late)
+        multiply_all(early[2:], grouped_early[2:], y_0, 0)
+        multiply_all(late, grouped_late, y_0, 0)
+        grouped_1 = interleave_all(PIECES[1])
+        scatter(y_0, 0)
+        multiply_all(PIECES[1], grouped_1, y_1, 1)
+        scatter(y_1, 1)
+
+        nc.sync.dma_start(out=out[:, 0 : T // 2], in_=window[:, 0 : T // 2])
+        nc.scalar.dma_start(out=out[:, T // 2 : T], in_=window[:, T // 2 : T])

@@ -21,11 +21,11 @@ S = 2048
 T = 4096
 HALF = S // 2
 
-LOADS = (((0, 512), (512, 256), (768, 256)), ((1024, 512), (1536, 256), (1792, 256)))
-PIECES = (
-    ((0, 256, "v"), (256, 256, "s"), (512, 128, "v"), (640, 128, "s"), (768, 128, "v"), (896, 128, "s")),
-    ((1024, 256, "s"), (1280, 256, "s"), (1536, 256, "s"), (1792, 256, "s")),
+STAGES = (
+    (((0, 256, "v"), (256, 256, "s")), ((0, 256), (256, 256))),
+    (((512, 256, "v"), (768, 128, "s"), (896, 128, "s")), ((768, 128), (512, 256), (896, 128))),
 )
+LOADS = (((0, 512), (512, 512)), ((1024, 512), (1536, 256), (1792, 256)))
 
 
 def tile_list_hscat_bias_kernel(tc, x, w_words, w_scales, b, wgo, offs, out):
@@ -38,7 +38,9 @@ def tile_list_hscat_bias_kernel(tc, x, w_words, w_scales, b, wgo, offs, out):
         window = held.tile([P, T], F32, name="window")
         w_codes = held.tile([P, 2 * P], U8, name="w_codes", align_bytes=64)
         w_plane = held.tile([P, P], U8, name="w_plane", align_bytes=64)
-        b_col = held.tile([P, 1], F32, name="b_col")
+        b_rows = held.tile([P, 32], F32, name="b_rows", align_bytes=64)
+        b_turned = held.tile([P, 32], F32, name="b_turned", align_bytes=64)
+        b_col = b_turned[:, 0:1]
         warm = held.tile([P, 1], F32, name="warm")
 
         x_view = x.rearrange("(p j) s -> p j s", j=PACK)
@@ -46,48 +48,55 @@ def tile_list_hscat_bias_kernel(tc, x, w_words, w_scales, b, wgo, offs, out):
 
         def load_x(first, tokens):
             chunk = held.tile([P, PACK, tokens], F32, name="raw_%d" % first)
+            if first == 512:
+                nc.vector.memset(chunk[:, 0, 0:8], 0.0)
             nc.sync.dma_start(out=chunk[:], in_=x_view[:, :, first : first + tokens])
-            raw[first] = (chunk, tokens)
+            raw[first] = chunk
 
         nc.gpsimd.memset(w_plane[:].bitcast(I32), 0)
-        nc.gpsimd.dma_start(out=b_col[:], in_=b.rearrange("(p o) -> p o", o=1))
-        nc.vector.memset(warm[:], 0.0)
+        nc.gpsimd.memset(b_rows[:], 0.0)
+        nc.gpsimd.memset(warm[:], 0.0)
         nc.scalar.dma_start(out=w_codes[:].bitcast(I32), in_=w_words[0].bitcast(I32))
         for q in range(4):
             nc.scalar.dma_start(
                 out=w_plane[32 * q : 32 * q + 4, :].bitcast(I32), in_=w_scales[0, 4 * q : 4 * q + 4, :].bitcast(I32)
             )
+        nc.scalar.dma_start(out=b_rows[0:P:32, :], in_=b.rearrange("(q n) -> q n", n=32))
         nc.scalar.activation(warm[:], warm[:], IDENTITY)
-        nc.vector.memset(window[:], 0.0)
         for load in LOADS[0]:
             load_x(*load)
-        nc.sync.dma_start(offsets[:], offs)
+        nc.vector.memset(window[:], 0.0)
+        nc.vector.transpose(b_turned[:], b_rows[:])
+
         wgo_tiles = []
         for h in range(2):
-            if h == 1:
+            if h == 0:
+                nc.sync.dma_start(offsets[:], offs)
+            else:
                 for load in LOADS[1]:
                     load_x(*load)
             wgo_half = held.tile([P, HALF], F32, name="wgo_%d" % h)
             nc.sync.dma_start(out=wgo_half[:], in_=wgo[:, h * HALF : (h + 1) * HALF])
             wgo_tiles.append(wgo_half)
 
-        def interleave(first, tokens, engine):
+        def interleave(first, tokens, engine, grouped):
             base = max(c for c in raw if c <= first)
-            chunk = raw[base][0]
-            grouped = held.tile([P, tokens * PACK], BF16, name="grouped_%d" % first, align_bytes=64)
-            dst = grouped[:].rearrange("p (c i t) -> p c t i", i=4, t=PACK)
+            chunk = raw[base]
+            dst = grouped.rearrange("p (c i t) -> p c t i", i=4, t=PACK)
             src = chunk[:, :, first - base : first - base + tokens].rearrange("p t (c i) -> p c t i", i=4)
             if engine == "v":
                 nc.vector.tensor_copy(out=dst, in_=src)
             else:
                 nc.scalar.copy(out=dst, in_=src)
-            return grouped
 
-        def multiply(first, tokens, grouped, y, column):
+        def new_grouped(first, tokens):
+            return held.tile([P, tokens * PACK], BF16, name="grouped_%d" % first, align_bytes=64)
+
+        def multiply(first, tokens, grouped):
+            acc = psum.tile([P, 512], F32, name="acc")
             codes = held.tile([P, tokens], U32, name="codes_%d" % first, align_bytes=64)
             plane = held.tile([P, tokens], U8, name="plane_%d" % first, align_bytes=64)
             nc.vector.quantize_mx(out=codes[:].bitcast(FP8X4), scales=plane[:], in_=grouped[:])
-            acc = psum.tile([P, 512], F32, name="acc")
             nc.tensor.matmul_mx(
                 out=acc[:, 0:tokens],
                 lhsT=w_codes[:].bitcast(FP4X4),
@@ -97,14 +106,10 @@ def tile_list_hscat_bias_kernel(tc, x, w_words, w_scales, b, wgo, offs, out):
                 start=True,
                 stop=True,
             )
-            nc.scalar.activation(y[:, column : column + tokens], acc[:, 0:tokens], IDENTITY, bias=b_col[:])
+            return acc[:, 0:tokens]
 
-        def interleave_all(pieces):
-            return [interleave(*piece) for piece in pieces]
-
-        def multiply_all(pieces, grouped, y, h):
-            for (first, tokens, engine), tile in zip(pieces, grouped):
-                multiply(first, tokens, tile, y, first - h * HALF)
+        def empty(y, acc):
+            nc.scalar.activation(y, acc, IDENTITY, bias=b_col)
 
         def scatter(y, h):
             nc.vector.tensor_tensor(
@@ -113,15 +118,33 @@ def tile_list_hscat_bias_kernel(tc, x, w_words, w_scales, b, wgo, offs, out):
 
         y_0 = held.tile([P, HALF], F32, name="y_0")
         y_1 = held.tile([P, HALF], F32, name="y_1")
-        early, late = PIECES[0][:4], PIECES[0][4:]
-        grouped_early = interleave_all(early)
-        multiply_all(early[:2], grouped_early[:2], y_0, 0)
-        grouped_late = interleave_all(late)
-        multiply_all(early[2:], grouped_early[2:], y_0, 0)
-        multiply_all(late, grouped_late, y_0, 0)
-        grouped_1 = interleave_all(PIECES[1])
+
+        for stage in STAGES:
+            tiles = {}
+            for first, tokens, engine in stage[0]:
+                tiles[first] = new_grouped(first, tokens)
+                interleave(first, tokens, engine, tiles[first][:])
+            for first, tokens in stage[1]:
+                acc = multiply(first, tokens, tiles[first])
+                empty(y_0[:, first : first + tokens], acc)
+
+        joined = {}
+        for near, far in ((1, 2), (0, 3)):
+            for part in range(2):
+                joined[near, part] = joined[far, part] = new_grouped(HALF + 256 * near + 128 * part, 256)
+        for block in range(4):
+            for part in range(2):
+                side = 512 * (block >= 2)
+                interleave(HALF + 256 * block + 128 * part, 128, "s", joined[block, part][:, side : side + 512])
         scatter(y_0, 0)
-        multiply_all(PIECES[1], grouped_1, y_1, 1)
+        y_view = y_1[:].rearrange("p (block n) -> p block n", block=4)
+        for near, far in ((1, 2), (0, 3)):
+            for part in range(2):
+                acc = multiply(HALF + 256 * near + 128 * part, 256, joined[near, part])
+                empty(
+                    y_view[:, near : far + 1 : far - near, 128 * part : 128 * (part + 1)],
+                    acc.rearrange("p (k n) -> p k n", k=2),
+                )
         scatter(y_1, 1)
 
         nc.sync.dma_start(out=out[:, 0 : T // 2], in_=window[:, 0 : T // 2])

from contextlib import ExitStack

import concourse.mybir as mybir

FLOPS = 2 * 512 * 128 * 2048

F32 = mybir.dt.float32
BF16 = mybir.dt.bfloat16
U32 = mybir.dt.uint32
I32 = mybir.dt.int32
U16 = mybir.dt.uint16
U8 = mybir.dt.uint8
FP8X4 = mybir.dt.float8_e4m3fn_x4
FP4X4 = mybir.dt.float4_e2m1fn_x4
MULT = mybir.AluOpType.mult
IDENTITY = mybir.ActivationFunctionType.Identity

P = 128
PACK = 4
S = 2048
T = 4096
HALF = S // 2

STAGES = (
    (((0, 256, "v"), (256, 256, "s")), ((0, 256), (256, 256))),
    (((512, 256, "v"), (768, 128, "s"), (896, 128, "s")), ((768, 128), (512, 256), (896, 128))),
)
LOADS = (((0, 512), (512, 512)), ((1024, 512), (1536, 256), (1792, 256)))


def tile_list_hscat_bias_kernel(tc, x, w_words, w_scales, b, wgo, offs, out):
    nc = tc.nc
    with ExitStack() as ctx:
        held = ctx.enter_context(tc.tile_pool(name="held", bufs=1))
        psum = ctx.enter_context(tc.psum_pool(name="psum", bufs=8))

        offsets = held.tile([P, S // 16], U16, name="offsets")
        window = held.tile([P, T], F32, name="window")
        w_codes = held.tile([P, 2 * P], U8, name="w_codes", align_bytes=64)
        w_plane = held.tile([P, P], U8, name="w_plane", align_bytes=64)
        b_rows = held.tile([P, 32], F32, name="b_rows", align_bytes=64)
        b_turned = held.tile([P, 32], F32, name="b_turned", align_bytes=64)
        b_col = b_turned[:, 0:1]
        warm = held.tile([P, 1], F32, name="warm")

        x_view = x.rearrange("(p j) s -> p j s", j=PACK)
        raw = {}

        def load_x(first, tokens):
            chunk = held.tile([P, PACK, tokens], F32, name="raw_%d" % first)
            if first == 512:
                nc.vector.memset(chunk[:, 0, 0:8], 0.0)
            nc.sync.dma_start(out=chunk[:], in_=x_view[:, :, first : first + tokens])
            raw[first] = chunk

        nc.gpsimd.memset(w_plane[:].bitcast(I32), 0)
        nc.gpsimd.memset(b_rows[:], 0.0)
        nc.gpsimd.memset(warm[:], 0.0)
        nc.scalar.dma_start(out=w_codes[:].bitcast(I32), in_=w_words[0].bitcast(I32))
        for q in range(4):
            nc.scalar.dma_start(
                out=w_plane[32 * q : 32 * q + 4, :].bitcast(I32), in_=w_scales[0, 4 * q : 4 * q + 4, :].bitcast(I32)
            )
        nc.scalar.dma_start(out=b_rows[0:P:32, :], in_=b.rearrange("(q n) -> q n", n=32))
        nc.scalar.activation(warm[:], warm[:], IDENTITY)
        for load in LOADS[0]:
            load_x(*load)
        nc.vector.memset(window[:], 0.0)
        nc.vector.transpose(b_turned[:], b_rows[:])

        wgo_tiles = []
        for h in range(2):
            if h == 0:
                nc.sync.dma_start(offsets[:], offs)
            else:
                for load in LOADS[1]:
                    load_x(*load)
            wgo_half = held.tile([P, HALF], F32, name="wgo_%d" % h)
            nc.sync.dma_start(out=wgo_half[:], in_=wgo[:, h * HALF : (h + 1) * HALF])
            wgo_tiles.append(wgo_half)

        def interleave(first, tokens, engine, grouped):
            base = max(c for c in raw if c <= first)
            chunk = raw[base]
            dst = grouped.rearrange("p (c i t) -> p c t i", i=4, t=PACK)
            src = chunk[:, :, first - base : first - base + tokens].rearrange("p t (c i) -> p c t i", i=4)
            if engine == "v":
                nc.vector.tensor_copy(out=dst, in_=src)
            else:
                nc.scalar.copy(out=dst, in_=src)

        def new_grouped(first, tokens):
            return held.tile([P, tokens * PACK], BF16, name="grouped_%d" % first, align_bytes=64)

        def multiply(first, tokens, grouped):
            acc = psum.tile([P, 512], F32, name="acc")
            codes = held.tile([P, tokens], U32, name="codes_%d" % first, align_bytes=64)
            plane = held.tile([P, tokens], U8, name="plane_%d" % first, align_bytes=64)
            nc.vector.quantize_mx(out=codes[:].bitcast(FP8X4), scales=plane[:], in_=grouped[:])
            nc.tensor.matmul_mx(
                out=acc[:, 0:tokens],
                lhsT=w_codes[:].bitcast(FP4X4),
                lhsT_scale=w_plane[:],
                rhs=codes[:].bitcast(FP8X4),
                rhs_scale=plane[:],
                start=True,
                stop=True,
            )
            return acc[:, 0:tokens]

        def empty(y, acc):
            nc.scalar.activation(y, acc, IDENTITY, bias=b_col)

        def scatter(y, h):
            nc.vector.tensor_tensor(
                window[:].indirect(offsets[:, h * 64 : (h + 1) * 64]), y[:], wgo_tiles[h][:], MULT
            )

        y_0 = held.tile([P, HALF], F32, name="y_0")
        y_1 = held.tile([P, HALF], F32, name="y_1")

        for stage in STAGES:
            tiles = {}
            for first, tokens, engine in stage[0]:
                tiles[first] = new_grouped(first, tokens)
                interleave(first, tokens, engine, tiles[first][:])
            for first, tokens in stage[1]:
                acc = multiply(first, tokens, tiles[first])
                empty(y_0[:, first : first + tokens], acc)

        joined = {}
        for near, far in ((1, 2), (0, 3)):
            for part in range(2):
                joined[near, part] = joined[far, part] = new_grouped(HALF + 256 * near + 128 * part, 256)
        for block in range(4):
            for part in range(2):
                side = 512 * (block >= 2)
                interleave(HALF + 256 * block + 128 * part, 128, "s", joined[block, part][:, side : side + 512])
        scatter(y_0, 0)
        y_view = y_1[:].rearrange("p (block n) -> p block n", block=4)
        for near, far in ((1, 2), (0, 3)):
            for part in range(2):
                acc = multiply(HALF + 256 * near + 128 * part, 256, joined[near, part])
                empty(
                    y_view[:, near : far + 1 : far - near, 128 * part : 128 * (part + 1)],
                    acc.rearrange("p (k n) -> p k n", k=2),
                )
        scatter(y_1, 1)

        nc.sync.dma_start(out=out[:, 0 : T // 2], in_=window[:, 0 : T // 2])
        nc.scalar.dma_start(out=out[:, T // 2 : T], in_=window[:, T // 2 : T])
